import numpy as np
import ml_dtypes


def mxq(x, axis, fmt="e4m3"):
    dtype, down = {"e4m3": (ml_dtypes.float8_e4m3fn, 7), "e5m2": (ml_dtypes.float8_e5m2, 14)}[fmt]
    v = np.moveaxis(np.asarray(x, np.float32).astype(ml_dtypes.bfloat16).astype(np.float64), axis, -1)
    blocks = v.reshape(v.shape[:-1] + (-1, 32))
    amax = np.abs(blocks).max(-1, keepdims=True)
    byte = np.maximum(np.where(amax > 0, np.frexp(amax)[1] - 1 + 127, 0) - down, 1)
    scale = np.exp2(byte - 127.0)
    codes = (blocks / scale).astype(np.float32).astype(dtype).astype(np.float64)
    return np.moveaxis((codes * scale).reshape(v.shape), -1, axis)


WIDE = False


def mx_kscale(k):
    if not WIDE:
        return np.ones(k)
    levels = np.array([10, -10, 5, -5, 0])
    if k % 512:
        return np.exp2(np.random.permutation(np.resize(levels, k // 32))).repeat(32)
    a = np.empty((k // 512, 16))
    for p in range(k // 512):
        a[p, :8] = np.random.permutation(np.resize(levels, 8))
        for g in range(8):
            far = levels[np.abs(levels - a[p, g]) >= 10]
            a[p, g + 8] = far[np.random.randint(len(far))]
    return np.exp2(a.ravel()).repeat(32)


def f64(x):
    return np.asarray(x).astype(np.float64)


def striped(idx):
    return np.tile(idx.reshape(-1, 16).T, (8, 1)).astype(np.uint16)


def unstriped(offs):
    return offs[:16].T.reshape(-1).astype(np.int64)


E2M1 = np.array([0.0, 0.5, 1.0, 1.5, 2.0, 3.0, 4.0, 6.0, -0.0, -0.5, -1.0, -1.5, -2.0, -3.0, -4.0, -6.0])


def pack_weight(w, fmt):
    k, n = w.shape
    w = f64(np.asarray(w, np.float32).astype(ml_dtypes.bfloat16)).reshape(k // 32, 32, n)
    amax = np.abs(w).max(1)
    if fmt == "e4m3":
        byte = np.frexp(amax)[1] - 1 + 127 - 7
    else:
        mant, ex = np.frexp(amax / 6.0)
        byte = np.where(mant > 0.5, ex, ex - 1) + 127
    byte = np.clip(np.where(amax > 0, byte, 1), 1, 254)
    scaled = (w * np.exp2(127.0 - byte)[:, None, :]).reshape(k, n).astype(np.float32)
    by_word = np.ascontiguousarray(scaled.reshape(k // 512, 128, 4, n).transpose(0, 1, 3, 2))
    if fmt == "e4m3":
        words = by_word.astype(ml_dtypes.float8_e4m3fn).view(np.uint8)
    else:
        c = by_word.astype(ml_dtypes.float4_e2m1fn).view(np.uint8) & 0xF
        words = (c[..., 0::2] | (c[..., 1::2] << 4)).reshape(k // 512, 128, 2 * n)
    return np.ascontiguousarray(words), np.ascontiguousarray(byte.astype(np.uint8).reshape(k // 512, 16, n))


def unpack_weight(words, scales, fmt):
    g, _, n = scales.shape
    words = np.ascontiguousarray(words).reshape(g, 128, n, -1)
    if fmt == "e4m3":
        vals = words.view(ml_dtypes.float8_e4m3fn).astype(np.float64)
    else:
        nib = np.empty((g, 128, n, 4), np.uint8)
        nib[..., 0::2] = words & 0xF
        nib[..., 1::2] = words >> 4
        vals = E2M1[nib]
    vals = vals * np.repeat(np.exp2(scales.astype(np.float64) - 127.0), 8, axis=1)[..., None]
    return vals.transpose(0, 1, 3, 2).reshape(g * 512, n)


def sigmoid(v):
    return 1.0 / (1.0 + np.exp(-np.maximum(v, -700.0)))


K, T, E, C, N = 1024, 1024, 8, 128, 512


def by_slot(wq, xq):
    return np.concatenate([xq[:, e * C:(e + 1) * C].T @ wq[e] for e in range(E)])


def setup_inputs():
    n = np.random.standard_normal
    s = mx_kscale(K)
    slot_token = np.concatenate([np.random.permutation(T)[:C] for e in range(E)])
    x = pack_weight(n((K, T)) * s[:, None], "e2m1")
    two = np.ascontiguousarray(x[0].reshape(K // 1024, 2, 128, T, 2).transpose(0, 2, 3, 1, 4).reshape(K // 1024, 128, T, 4))
    return {
        "x_words": two,
        "x_scales": x[1],
        "w": (n((E, K, N)) / np.sqrt(K) / s[None, :, None]).astype(np.float32),
        "w3": (n((E, K, N)) / np.sqrt(K) / s[None, :, None]).astype(np.float32),
        "offs": striped(slot_token),
    }


def reference(x_words, x_scales, w, w3, offs):
    wq = mxq(f64(w), 1, "e4m3")
    w3q = mxq(f64(w3), 1, "e4m3")
    idx = unstriped(offs)
    words = x_words.reshape(K // 1024, 128, T, 2, 2).transpose(0, 3, 1, 2, 4).reshape(K // 512, 128, 2 * T)
    xq = unpack_weight(words, x_scales, "e2m1")[:, idx]
    y = sigmoid(by_slot(wq, xq)) * by_slot(w3q, xq)
    return y

@@ -1,0 +1,138 @@
+from contextlib import ExitStack
+
+import concourse.mybir as mybir
+
+K, T, E, C, N = 1024, 1024, 8, 128, 512
+FLOPS = 2 * 2 * E * C * K * N
+
+F32 = mybir.dt.float32
+BF16 = mybir.dt.bfloat16
+I32 = mybir.dt.int32
+U32 = mybir.dt.uint32
+U16 = mybir.dt.uint16
+U8 = mybir.dt.uint8
+FP8X4 = mybir.dt.float8_e4m3fn_x4
+FP4X4 = mybir.dt.float4_e2m1fn_x4
+
+P = 128
+PACK = 4
+K_PASS = P * PACK
+PASSES = K // K_PASS
+SLOTS = E * C
+GATHER = 512
+EXPERTS_PER_GATHER = GATHER // C
+VECTOR_COLS = 256
+RUN = 4
+RAW_RING = 16
+GROUPED_RING = 6
+CODE_RING = 6
+SUM_RING = 6
+STEPS = E * 2 * PASSES
+
+
+def tile_moe_s_glu_sigmoid_kernel(tc, x_words, x_scales, w, w3, offs, out):
+    nc = tc.nc
+    with ExitStack() as ctx:
+        keep = ctx.enter_context(tc.tile_pool(name="keep", bufs=1))
+        psum = ctx.enter_context(tc.psum_pool(name="psum", bufs=1))
+
+        offsets = keep.tile([P, SLOTS // 16], U16, name="offsets")
+        nc.sync.dma_start(offsets[:], offs)
+
+        token_words = keep.tile([P, T], I32, name="token_words")
+        nc.sync.dma_start(out=token_words[:], in_=x_words[0].rearrange("p t d -> p (t d)").bitcast(I32))
+
+        token_scales = keep.tile([P, PASSES * T], U8, name="token_scales")
+        nc.vector.memset(token_scales[:].bitcast(I32), 0)
+        scale_rows = token_scales[:].bitcast(I32).rearrange("p (s t) -> p s t", s=PASSES)
+        for quadrant in range(4):
+            nc.sync.dma_start(
+                out=scale_rows[32 * quadrant : 32 * quadrant + 4],
+                in_=x_scales[:, 4 * quadrant : 4 * quadrant + 4, :].bitcast(I32).rearrange("s b t -> b s t"),
+            )
+
+        results = keep.tile([P, E, N], F32, name="results")
+        raw_ring = [keep.tile([P, PACK, N], F32, name=f"raw{i}") for i in range(RAW_RING)]
+        grouped_ring = [keep.tile([P, N, PACK], BF16, name=f"grouped{i}", align_bytes=64) for i in range(GROUPED_RING)]
+        code_ring = [keep.tile([P, N], U32, name=f"codes{i}", align_bytes=64) for i in range(CODE_RING)]
+        scale_ring = [keep.tile([P, N], U8, name=f"scales{i}", align_bytes=64) for i in range(CODE_RING)]
+        sum_ring = [psum.tile([C, N], F32, name=f"sums{i}") for i in range(SUM_RING)]
+
+        def gather_slots(part):
+            picked = offsets[:, part * GATHER // 16 : (part + 1) * GATHER // 16]
+            pair_words = keep.tile([P, GATHER], U32, name=f"pair_words{part}")
+            nc.vector.tensor_copy(pair_words[:], token_words[:].bitcast(U32).indirect(picked))
+            slot_scales = keep.tile([P, PASSES, GATHER], U8, name=f"slot_scales{part}", align_bytes=64)
+            for s in range(PASSES):
+                nc.vector.tensor_copy(slot_scales[:, s, :], token_scales[:, s * T : (s + 1) * T].indirect(picked))
+            slot_words = keep.tile([P, PASSES, 2 * GATHER], U8, name=f"slot_words{part}", align_bytes=64)
+            nc.vector.tensor_copy(
+                slot_words[:].bitcast(U16),
+                pair_words[:].bitcast(U16).rearrange("p (j s) -> p s j", s=PASSES),
+            )
+            return slot_words, slot_scales
+
+        def quantize_pass(step, rows):
+            raw = raw_ring[step % RAW_RING]
+            nc.sync.dma_start(out=raw[:], in_=rows.rearrange("(p j) n -> p j n", j=PACK))
+            grouped = grouped_ring[step % GROUPED_RING]
+            src = raw[:].rearrange("p j (c i) -> p c j i", i=RUN)
+            dst = grouped[:].rearrange("p (c i) j -> p c j i", i=RUN)
+            cut = VECTOR_COLS // RUN
+            nc.vector.tensor_copy(out=dst[:, :cut], in_=src[:, :cut])
+            nc.scalar.copy(out=dst[:, cut:], in_=src[:, cut:])
+            codes, scales = code_ring[step % CODE_RING], scale_ring[step % CODE_RING]
+            nc.vector.quantize_mx(
+                out=codes[:].bitcast(FP8X4),
+                scales=scales[:],
+                in_=grouped[:].rearrange("p n j -> p (n j)"),
+            )
+            return codes, scales
+
+        out_rows = out.rearrange("(e u) n -> u e n", u=C)
+
+        def gate_step(e):
+            return min(2 * PASSES * (e + 1) + 1, STEPS - 2)
+
+        def gate_tile(e):
+            return raw_ring[gate_step(e) % RAW_RING][:, 0, :]
+
+        def make_gate(e):
+            nc.scalar.activation(
+                out=gate_tile(e), in_=sum_ring[2 * e % SUM_RING][:], func=mybir.ActivationFunctionType.Sigmoid
+            )
+
+        def apply_gate(e):
+            nc.vector.tensor_tensor(
+                out=results[:, e, :],
+                in0=sum_ring[(2 * e + 1) % SUM_RING][:],
+                in1=gate_tile(e),
+                op=mybir.AluOpType.mult,
+            )
+
+        for e in range(E):
+            if e % EXPERTS_PER_GATHER == 0:
+                slot_words, slot_scales = gather_slots(e // EXPERTS_PER_GATHER)
+            first = (e % EXPERTS_PER_GATHER) * C
+            for which, weight in enumerate((w, w3)):
+                sums = sum_ring[(2 * e + which) % SUM_RING]
+                for s in range(PASSES):
+                    step = (2 * e + which) * PASSES + s
+                    codes, scales = quantize_pass(step, weight[e, s * K_PASS : (s + 1) * K_PASS, :])
+                    nc.tensor.matmul_mx(
+                        out=sums[:],
+                        lhsT=slot_words[:, s, 2 * first : 2 * (first + C)].bitcast(FP4X4),
+                        lhsT_scale=slot_scales[:, s, first : first + C],
+                        rhs=codes[:].bitcast(FP8X4),
+                        rhs_scale=scales[:],
+                        start=(s == 0),
+                        stop=(s == PASSES - 1),
+                    )
+                    if e > 0 and step == gate_step(e - 1):
+                        make_gate(e - 1)
+                        apply_gate(e - 1)
+                    if step == gate_step(E - 1):
+                        make_gate(E - 1)
+        nc.sync.dma_start(out=out_rows[:, : E - 1, :], in_=results[:, : E - 1, :])
+        apply_gate(E - 1)
+        nc.sync.dma_start(out=out_rows[:, E - 1, :], in_=results[:, E - 1, :])

@@ -22,8 +22,9 @@ SLOTS = E * C
 GATHER = 512
 EXPERTS_PER_GATHER = GATHER // C
 VECTOR_COLS = 256
+LAST_VECTOR_COLS = 352
 RUN = 4
-RAW_RING = 16
+RAW_RING = 9
 GROUPED_RING = 6
 CODE_RING = 6
 SUM_RING = 6
@@ -37,10 +38,31 @@ def tile_moe_s_glu_sigmoid_kernel(tc, x_words, x_scales, w, w3, offs, out):
         psum = ctx.enter_context(tc.psum_pool(name="psum", bufs=1))
 
         offsets = keep.tile([P, SLOTS // 16], U16, name="offsets")
-        nc.sync.dma_start(offsets[:], offs)
+
+        results = keep.tile([P, E, N], F32, name="results")
+        raw_ring = [keep.tile([P, PASSES, PACK, N], F32, name=f"raw{i}") for i in range(RAW_RING)]
+        grouped_ring = [keep.tile([P, N, PACK], BF16, name=f"grouped{i}", align_bytes=64) for i in range(GROUPED_RING)]
+        code_ring = [keep.tile([P, N], U32, name=f"codes{i}", align_bytes=64) for i in range(CODE_RING)]
+        scale_ring = [keep.tile([P, N], U8, name=f"scales{i}", align_bytes=64) for i in range(CODE_RING)]
+        sum_ring = [psum.tile([C, N], F32, name=f"sums{i}") for i in range(SUM_RING)]
+
+        def raw_pass(step):
+            return raw_ring[step // PASSES % RAW_RING][:, step % PASSES]
+
+        def load_matrix(e, which):
+            rows = (w, w3)[which][e].rearrange("(s p j) n -> p s j n", s=PASSES, j=PACK)
+            raw = raw_ring[(2 * e + which) % RAW_RING]
+            if e < E - 1:
+                nc.sync.dma_start(out=raw[:], in_=rows)
+            else:
+                for s in range(PASSES):
+                    nc.sync.dma_start(out=raw[:, s], in_=rows[:, s])
 
         token_words = keep.tile([P, T], I32, name="token_words")
         nc.sync.dma_start(out=token_words[:], in_=x_words[0].rearrange("p t d -> p (t d)").bitcast(I32))
+        nc.sync.dma_start(offsets[:], offs)
+        load_matrix(0, 0)
+
 
         token_scales = keep.tile([P, PASSES * T], U8, name="token_scales")
         nc.vector.memset(token_scales[:].bitcast(I32), 0)
@@ -50,13 +72,6 @@ def tile_moe_s_glu_sigmoid_kernel(tc, x_words, x_scales, w, w3, offs, out):
                 out=scale_rows[32 * quadrant : 32 * quadrant + 4],
                 in_=x_scales[:, 4 * quadrant : 4 * quadrant + 4, :].bitcast(I32).rearrange("s b t -> b s t"),
             )
-
-        results = keep.tile([P, E, N], F32, name="results")
-        raw_ring = [keep.tile([P, PACK, N], F32, name=f"raw{i}") for i in range(RAW_RING)]
-        grouped_ring = [keep.tile([P, N, PACK], BF16, name=f"grouped{i}", align_bytes=64) for i in range(GROUPED_RING)]
-        code_ring = [keep.tile([P, N], U32, name=f"codes{i}", align_bytes=64) for i in range(CODE_RING)]
-        scale_ring = [keep.tile([P, N], U8, name=f"scales{i}", align_bytes=64) for i in range(CODE_RING)]
-        sum_ring = [psum.tile([C, N], F32, name=f"sums{i}") for i in range(SUM_RING)]
 
         def gather_slots(part):
             picked = offsets[:, part * GATHER // 16 : (part + 1) * GATHER // 16]
@@ -72,13 +87,12 @@ def tile_moe_s_glu_sigmoid_kernel(tc, x_words, x_scales, w, w3, offs, out):
             )
             return slot_words, slot_scales
 
-        def quantize_pass(step, rows):
-            raw = raw_ring[step % RAW_RING]
-            nc.sync.dma_start(out=raw[:], in_=rows.rearrange("(p j) n -> p j n", j=PACK))
+        def quantize_pass(step):
+            raw = raw_pass(step)
             grouped = grouped_ring[step % GROUPED_RING]
-            src = raw[:].rearrange("p j (c i) -> p c j i", i=RUN)
+            src = raw.rearrange("p j (c i) -> p c j i", i=RUN)
             dst = grouped[:].rearrange("p (c i) j -> p c j i", i=RUN)
-            cut = VECTOR_COLS // RUN
+            cut = (LAST_VECTOR_COLS if step == STEPS - 1 else VECTOR_COLS) // RUN
             nc.vector.tensor_copy(out=dst[:, :cut], in_=src[:, :cut])
             nc.scalar.copy(out=dst[:, cut:], in_=src[:, cut:])
             codes, scales = code_ring[step % CODE_RING], scale_ring[step % CODE_RING]
@@ -92,10 +106,10 @@ def tile_moe_s_glu_sigmoid_kernel(tc, x_words, x_scales, w, w3, offs, out):
         out_rows = out.rearrange("(e u) n -> u e n", u=C)
 
         def gate_step(e):
-            return min(2 * PASSES * (e + 1) + 1, STEPS - 2)
+            return min(2 * PASSES * (e + 1), STEPS - 2)
 
         def gate_tile(e):
-            return raw_ring[gate_step(e) % RAW_RING][:, 0, :]
+            return raw_pass(gate_step(e))[:, 0, :]
 
         def make_gate(e):
             nc.scalar.activation(
@@ -114,11 +128,13 @@ def tile_moe_s_glu_sigmoid_kernel(tc, x_words, x_scales, w, w3, offs, out):
             if e % EXPERTS_PER_GATHER == 0:
                 slot_words, slot_scales = gather_slots(e // EXPERTS_PER_GATHER)
             first = (e % EXPERTS_PER_GATHER) * C
-            for which, weight in enumerate((w, w3)):
+            for which in range(2):
+                if (e, which) != (0, 0):
+                    load_matrix(e, which)
                 sums = sum_ring[(2 * e + which) % SUM_RING]
                 for s in range(PASSES):
                     step = (2 * e + which) * PASSES + s
-                    codes, scales = quantize_pass(step, weight[e, s * K_PASS : (s + 1) * K_PASS, :])
+                    codes, scales = quantize_pass(step)
                     nc.tensor.matmul_mx(
                         out=sums[:],
                         lhsT=slot_words[:, s, 2 * first : 2 * (first + C)].bitcast(FP4X4),

@@ -39,8 +39,8 @@ def tile_moe_s_glu_sigmoid_kernel(tc, x_words, x_scales, w, w3, offs, out):
 
         offsets = keep.tile([P, SLOTS // 16], U16, name="offsets")
 
-        results = keep.tile([P, E, N], F32, name="results")
-        raw_ring = [keep.tile([P, PASSES, PACK, N], F32, name=f"raw{i}") for i in range(RAW_RING)]
+        results = keep.tile([P, E, N], F32, name="results", align_bytes=256)
+        raw_ring = [keep.tile([P, PASSES, PACK, N], F32, name=f"raw{i}", align_bytes=256) for i in range(RAW_RING)]
         grouped_ring = [keep.tile([P, N, PACK], BF16, name=f"grouped{i}", align_bytes=64) for i in range(GROUPED_RING)]
         code_ring = [keep.tile([P, N], U32, name=f"codes{i}", align_bytes=64) for i in range(CODE_RING)]
         scale_ring = [keep.tile([P, N], U8, name=f"scales{i}", align_bytes=64) for i in range(CODE_RING)]
@@ -58,13 +58,13 @@ def tile_moe_s_glu_sigmoid_kernel(tc, x_words, x_scales, w, w3, offs, out):
                 for s in range(PASSES):
                     nc.sync.dma_start(out=raw[:, s], in_=rows[:, s])
 
-        token_words = keep.tile([P, T], I32, name="token_words")
+        token_words = keep.tile([P, T], I32, name="token_words", align_bytes=256)
         nc.sync.dma_start(out=token_words[:], in_=x_words[0].rearrange("p t d -> p (t d)").bitcast(I32))
         nc.sync.dma_start(offsets[:], offs)
         load_matrix(0, 0)
 
 
-        token_scales = keep.tile([P, PASSES * T], U8, name="token_scales")
+        token_scales = keep.tile([P, PASSES * T], U8, name="token_scales", align_bytes=256)
         nc.vector.memset(token_scales[:].bitcast(I32), 0)
         scale_rows = token_scales[:].bitcast(I32).rearrange("p (s t) -> p s t", s=PASSES)
         for quadrant in range(4):

@@ -22,12 +22,14 @@ SLOTS = E * C
 GATHER = 512
 EXPERTS_PER_GATHER = GATHER // C
 VECTOR_COLS = 256
-LAST_VECTOR_COLS = 352
+TAIL_COLS = 128
+TAIL_PARTS = N // TAIL_COLS
+TAIL_VECTOR_PARTS = 2
 RUN = 4
 RAW_RING = 9
 GROUPED_RING = 6
 CODE_RING = 6
-SUM_RING = 6
+SUM_RING = 4
 STEPS = E * 2 * PASSES
 
 
@@ -45,6 +47,8 @@ def tile_moe_s_glu_sigmoid_kernel(tc, x_words, x_scales, w, w3, offs, out):
         code_ring = [keep.tile([P, N], U32, name=f"codes{i}", align_bytes=64) for i in range(CODE_RING)]
         scale_ring = [keep.tile([P, N], U8, name=f"scales{i}", align_bytes=64) for i in range(CODE_RING)]
         sum_ring = [psum.tile([C, N], F32, name=f"sums{i}") for i in range(SUM_RING)]
+
+        tail_sums = [psum.tile([C, TAIL_COLS], F32, name=f"tail_sums{g}") for g in range(TAIL_PARTS)]
 
         def raw_pass(step):
             return raw_ring[step // PASSES % RAW_RING][:, step % PASSES]
@@ -87,21 +91,37 @@ def tile_moe_s_glu_sigmoid_kernel(tc, x_words, x_scales, w, w3, offs, out):
             )
             return slot_words, slot_scales
 
-        def quantize_pass(step):
-            raw = raw_pass(step)
-            grouped = grouped_ring[step % GROUPED_RING]
-            src = raw.rearrange("p j (c i) -> p c j i", i=RUN)
-            dst = grouped[:].rearrange("p (c i) j -> p c j i", i=RUN)
-            cut = (LAST_VECTOR_COLS if step == STEPS - 1 else VECTOR_COLS) // RUN
-            nc.vector.tensor_copy(out=dst[:, :cut], in_=src[:, :cut])
-            nc.scalar.copy(out=dst[:, cut:], in_=src[:, cut:])
-            codes, scales = code_ring[step % CODE_RING], scale_ring[step % CODE_RING]
-            nc.vector.quantize_mx(
-                out=codes[:].bitcast(FP8X4),
-                scales=scales[:],
-                in_=grouped[:].rearrange("p n j -> p (n j)"),
+        def round_columns(copy, step, cols):
+            copy(
+                out=grouped_ring[step % GROUPED_RING][:, cols, :].rearrange("p (c i) j -> p c j i", i=RUN),
+                in_=raw_pass(step)[:, :, cols].rearrange("p j (c i) -> p c j i", i=RUN),
             )
-            return codes, scales
+
+        def quantize_columns(step, cols):
+            nc.vector.quantize_mx(
+                out=code_ring[step % CODE_RING][:, cols].bitcast(FP8X4),
+                scales=scale_ring[step % CODE_RING][:, cols],
+                in_=grouped_ring[step % GROUPED_RING][:, cols, :].rearrange("p n j -> p (n j)"),
+            )
+
+        def quantize_pass(step):
+            round_columns(nc.vector.tensor_copy, step, slice(0, VECTOR_COLS))
+            round_columns(nc.scalar.copy, step, slice(VECTOR_COLS, N))
+            quantize_columns(step, slice(0, N))
+
+        def multiply(sums, slots, step, cols):
+            e, s = step // (2 * PASSES), step % PASSES
+            slot_words, slot_scales = slots
+            first = (e % EXPERTS_PER_GATHER) * C
+            nc.tensor.matmul_mx(
+                out=sums[:],
+                lhsT=slot_words[:, s, 2 * first : 2 * (first + C)].bitcast(FP4X4),
+                lhsT_scale=slot_scales[:, s, first : first + C],
+                rhs=code_ring[step % CODE_RING][:, cols].bitcast(FP8X4),
+                rhs_scale=scale_ring[step % CODE_RING][:, cols],
+                start=(s == 0),
+                stop=(s == PASSES - 1),
+            )
 
         out_rows = out.rearrange("(e u) n -> u e n", u=C)
 
@@ -116,39 +136,36 @@ def tile_moe_s_glu_sigmoid_kernel(tc, x_words, x_scales, w, w3, offs, out):
                 out=gate_tile(e), in_=sum_ring[2 * e % SUM_RING][:], func=mybir.ActivationFunctionType.Sigmoid
             )
 
-        def apply_gate(e):
+        def apply_gate(e, sums, cols):
             nc.vector.tensor_tensor(
-                out=results[:, e, :],
-                in0=sum_ring[(2 * e + 1) % SUM_RING][:],
-                in1=gate_tile(e),
-                op=mybir.AluOpType.mult,
+                out=results[:, e, cols], in0=sums[:], in1=gate_tile(e)[:, cols], op=mybir.AluOpType.mult
             )
 
-        for e in range(E):
-            if e % EXPERTS_PER_GATHER == 0:
-                slot_words, slot_scales = gather_slots(e // EXPERTS_PER_GATHER)
-            first = (e % EXPERTS_PER_GATHER) * C
-            for which in range(2):
-                if (e, which) != (0, 0):
-                    load_matrix(e, which)
-                sums = sum_ring[(2 * e + which) % SUM_RING]
-                for s in range(PASSES):
-                    step = (2 * e + which) * PASSES + s
-                    codes, scales = quantize_pass(step)
-                    nc.tensor.matmul_mx(
-                        out=sums[:],
-                        lhsT=slot_words[:, s, 2 * first : 2 * (first + C)].bitcast(FP4X4),
-                        lhsT_scale=slot_scales[:, s, first : first + C],
-                        rhs=codes[:].bitcast(FP8X4),
-                        rhs_scale=scales[:],
-                        start=(s == 0),
-                        stop=(s == PASSES - 1),
-                    )
-                    if e > 0 and step == gate_step(e - 1):
-                        make_gate(e - 1)
-                        apply_gate(e - 1)
-                    if step == gate_step(E - 1):
-                        make_gate(E - 1)
+        for step in range(STEPS - PASSES):
+            matrix, s = divmod(step, PASSES)
+            e, which = divmod(matrix, 2)
+            if step % (2 * PASSES * EXPERTS_PER_GATHER) == 0:
+                slots = gather_slots(e // EXPERTS_PER_GATHER)
+            if s == 0 and matrix > 0:
+                load_matrix(e, which)
+            quantize_pass(step)
+            multiply(sum_ring[matrix % SUM_RING], slots, step, slice(0, N))
+            if e > 0 and step == gate_step(e - 1):
+                make_gate(e - 1)
+                apply_gate(e - 1, sum_ring[(2 * e - 1) % SUM_RING], slice(0, N))
+
+        load_matrix(E - 1, 1)
         nc.sync.dma_start(out=out_rows[:, : E - 1, :], in_=results[:, : E - 1, :])
-        apply_gate(E - 1)
+        parts = [slice(g * TAIL_COLS, (g + 1) * TAIL_COLS) for g in range(TAIL_PARTS)]
+        quantize_pass(STEPS - 2)
+        for g, cols in enumerate(parts):
+            multiply(tail_sums[g], slots, STEPS - 2, cols)
+        make_gate(E - 1)
+        for g, cols in enumerate(parts):
+            round_columns(nc.vector.tensor_copy if g < TAIL_VECTOR_PARTS else nc.scalar.copy, STEPS - 1, cols)
+        for g in (0, 2, 1, 3):
+            quantize_columns(STEPS - 1, parts[g])
+            multiply(tail_sums[g], slots, STEPS - 1, parts[g])
+        for g in (0, 2, 1, 3):
+            apply_gate(E - 1, tail_sums[g], parts[g])
         nc.sync.dma_start(out=out_rows[:, E - 1, :], in_=results[:, E - 1, :])

@@ -26,7 +26,8 @@ TAIL_COLS = 128
 TAIL_PARTS = N // TAIL_COLS
 TAIL_VECTOR_PARTS = 2
 RUN = 4
-RAW_RING = 9
+RAW_SLOTS = 20
+GROUPS = ((0, 4), (4, 6), (6, 7), (7, 8))
 GROUPED_RING = 6
 CODE_RING = 6
 SUM_RING = 4
@@ -42,7 +43,7 @@ def tile_moe_s_glu_sigmoid_kernel(tc, x_words, x_scales, w, w3, offs, out):
         offsets = keep.tile([P, SLOTS // 16], U16, name="offsets")
 
         results = keep.tile([P, E, N], F32, name="results", align_bytes=256)
-        raw_ring = [keep.tile([P, PASSES, PACK, N], F32, name=f"raw{i}", align_bytes=256) for i in range(RAW_RING)]
+        raw = keep.tile([P, RAW_SLOTS, PACK, N], F32, name="raw", align_bytes=256)
         grouped_ring = [keep.tile([P, N, PACK], BF16, name=f"grouped{i}", align_bytes=64) for i in range(GROUPED_RING)]
         code_ring = [keep.tile([P, N], U32, name=f"codes{i}", align_bytes=64) for i in range(CODE_RING)]
         scale_ring = [keep.tile([P, N], U8, name=f"scales{i}", align_bytes=64) for i in range(CODE_RING)]
@@ -50,32 +51,42 @@ def tile_moe_s_glu_sigmoid_kernel(tc, x_words, x_scales, w, w3, offs, out):
 
         tail_sums = [psum.tile([C, TAIL_COLS], F32, name=f"tail_sums{g}") for g in range(TAIL_PARTS)]
 
-        def raw_pass(step):
-            return raw_ring[step // PASSES % RAW_RING][:, step % PASSES]
+        work = [
+            (e, which, s)
+            for first, last in GROUPS
+            for which in range(2)
+            for e in range(first, last)
+            for s in range(PASSES)
+        ]
+        step_of = {item: step for step, item in enumerate(work)}
 
-        def load_matrix(e, which):
-            rows = (w, w3)[which][e].rearrange("(s p j) n -> p s j n", s=PASSES, j=PACK)
-            raw = raw_ring[(2 * e + which) % RAW_RING]
-            if e < E - 1:
-                nc.sync.dma_start(out=raw[:], in_=rows)
+        def raw_pass(step):
+            return raw[:, step % RAW_SLOTS]
+
+        def load_group(first, last, which):
+            rows = (w, w3)[which][first:last].rearrange("e (s p j) n -> p (e s) j n", s=PASSES, j=PACK)
+            slot = step_of[(first, which, 0)] % RAW_SLOTS
+            if last < E:
+                nc.sync.dma_start(out=raw[:, slot : slot + PASSES * (last - first)], in_=rows)
             else:
                 for s in range(PASSES):
-                    nc.sync.dma_start(out=raw[:, s], in_=rows[:, s])
+                    nc.sync.dma_start(out=raw[:, slot + s], in_=rows[:, s])
 
         token_words = keep.tile([P, T], I32, name="token_words", align_bytes=256)
         nc.sync.dma_start(out=token_words[:], in_=x_words[0].rearrange("p t d -> p (t d)").bitcast(I32))
         nc.sync.dma_start(offsets[:], offs)
-        load_matrix(0, 0)
 
-
+        landed_scales = keep.tile([P, PASSES, T // 4], I32, name="landed_scales", align_bytes=256)
         token_scales = keep.tile([P, PASSES * T], U8, name="token_scales", align_bytes=256)
         nc.vector.memset(token_scales[:].bitcast(I32), 0)
         scale_rows = token_scales[:].bitcast(I32).rearrange("p (s t) -> p s t", s=PASSES)
         for quadrant in range(4):
+            live = slice(32 * quadrant, 32 * quadrant + 4)
             nc.sync.dma_start(
-                out=scale_rows[32 * quadrant : 32 * quadrant + 4],
+                out=landed_scales[live],
                 in_=x_scales[:, 4 * quadrant : 4 * quadrant + 4, :].bitcast(I32).rearrange("s b t -> b s t"),
             )
+            nc.vector.tensor_copy(scale_rows[live], landed_scales[live])
 
         def gather_slots(part):
             picked = offsets[:, part * GATHER // 16 : (part + 1) * GATHER // 16]
@@ -110,8 +121,8 @@ def tile_moe_s_glu_sigmoid_kernel(tc, x_words, x_scales, w, w3, offs, out):
             quantize_columns(step, slice(0, N))
 
         def multiply(sums, slots, step, cols):
-            e, s = step // (2 * PASSES), step % PASSES
-            slot_words, slot_scales = slots
+            e, which, s = work[step]
+            slot_words, slot_scales = slots[e // EXPERTS_PER_GATHER]
             first = (e % EXPERTS_PER_GATHER) * C
             nc.tensor.matmul_mx(
                 out=sums[:],
@@ -126,14 +137,14 @@ def tile_moe_s_glu_sigmoid_kernel(tc, x_words, x_scales, w, w3, offs, out):
         out_rows = out.rearrange("(e u) n -> u e n", u=C)
 
         def gate_step(e):
-            return min(2 * PASSES * (e + 1), STEPS - 2)
+            return step_of[(e, 0, PASSES - 1)] + 1
 
         def gate_tile(e):
             return raw_pass(gate_step(e))[:, 0, :]
 
         def make_gate(e):
             nc.scalar.activation(
-                out=gate_tile(e), in_=sum_ring[2 * e % SUM_RING][:], func=mybir.ActivationFunctionType.Sigmoid
+                out=gate_tile(e), in_=sum_ring[step_of[(e, 0, 0)] // PASSES % SUM_RING][:], func=mybir.ActivationFunctionType.Sigmoid
             )
 
         def apply_gate(e, sums, cols):
@@ -141,20 +152,26 @@ def tile_moe_s_glu_sigmoid_kernel(tc, x_words, x_scales, w, w3, offs, out):
                 out=results[:, e, cols], in0=sums[:], in1=gate_tile(e)[:, cols], op=mybir.AluOpType.mult
             )
 
-        for step in range(STEPS - PASSES):
-            matrix, s = divmod(step, PASSES)
-            e, which = divmod(matrix, 2)
-            if step % (2 * PASSES * EXPERTS_PER_GATHER) == 0:
-                slots = gather_slots(e // EXPERTS_PER_GATHER)
-            if s == 0 and matrix > 0:
-                load_matrix(e, which)
-            quantize_pass(step)
-            multiply(sum_ring[matrix % SUM_RING], slots, step, slice(0, N))
-            if e > 0 and step == gate_step(e - 1):
-                make_gate(e - 1)
-                apply_gate(e - 1, sum_ring[(2 * e - 1) % SUM_RING], slice(0, N))
+        starts = {step_of[(first, which, 0)]: (first, last, which) for first, last in GROUPS for which in range(2)}
+        load_group(*starts[0])
+        slots = [gather_slots(part) for part in range(SLOTS // GATHER)]
 
-        load_matrix(E - 1, 1)
+        def finish_matrix(step):
+            e, which, s = work[step]
+            if which == 0:
+                make_gate(e)
+            else:
+                apply_gate(e, sum_ring[step // PASSES % SUM_RING], slice(0, N))
+
+        for step in range(STEPS - PASSES):
+            if step > 0 and step in starts:
+                load_group(*starts[step])
+            quantize_pass(step)
+            multiply(sum_ring[step // PASSES % SUM_RING], slots, step, slice(0, N))
+            if step > 0 and step % PASSES == 0:
+                finish_matrix(step - 1)
+
+        load_group(*starts[STEPS - PASSES])
         nc.sync.dma_start(out=out_rows[:, : E - 1, :], in_=results[:, : E - 1, :])
         parts = [slice(g * TAIL_COLS, (g + 1) * TAIL_COLS) for g in range(TAIL_PARTS)]
         quantize_pass(STEPS - 2)

@@ -24,10 +24,10 @@ EXPERTS_PER_GATHER = GATHER // C
 VECTOR_COLS = 256
 TAIL_COLS = 128
 TAIL_PARTS = N // TAIL_COLS
-TAIL_VECTOR_PARTS = 2
+TAIL_LOADS = ((0, 2), (2, 3), (3, 4))
 RUN = 4
-RAW_SLOTS = 20
-GROUPS = ((0, 4), (4, 6), (6, 7), (7, 8))
+RAW_SLOTS = 18
+GROUPS = tuple((e, e + 1) for e in range(E))
 GROUPED_RING = 6
 CODE_RING = 6
 SUM_RING = 4
@@ -69,24 +69,24 @@ def tile_moe_s_glu_sigmoid_kernel(tc, x_words, x_scales, w, w3, offs, out):
             if last < E:
                 nc.sync.dma_start(out=raw[:, slot : slot + PASSES * (last - first)], in_=rows)
             else:
-                for s in range(PASSES):
+                for s in range(PASSES - which):
                     nc.sync.dma_start(out=raw[:, slot + s], in_=rows[:, s])
 
         token_words = keep.tile([P, T], I32, name="token_words", align_bytes=256)
         nc.sync.dma_start(out=token_words[:], in_=x_words[0].rearrange("p t d -> p (t d)").bitcast(I32))
         nc.sync.dma_start(offsets[:], offs)
 
-        landed_scales = keep.tile([P, PASSES, T // 4], I32, name="landed_scales", align_bytes=256)
+        starts = {step_of[(first, which, 0)]: (first, last, which) for first, last in GROUPS for which in range(2)}
+        load_group(*starts[0])
+
         token_scales = keep.tile([P, PASSES * T], U8, name="token_scales", align_bytes=256)
         nc.vector.memset(token_scales[:].bitcast(I32), 0)
         scale_rows = token_scales[:].bitcast(I32).rearrange("p (s t) -> p s t", s=PASSES)
         for quadrant in range(4):
-            live = slice(32 * quadrant, 32 * quadrant + 4)
             nc.sync.dma_start(
-                out=landed_scales[live],
+                out=scale_rows[32 * quadrant : 32 * quadrant + 4],
                 in_=x_scales[:, 4 * quadrant : 4 * quadrant + 4, :].bitcast(I32).rearrange("s b t -> b s t"),
             )
-            nc.vector.tensor_copy(scale_rows[live], landed_scales[live])
 
         def gather_slots(part):
             picked = offsets[:, part * GATHER // 16 : (part + 1) * GATHER // 16]
@@ -102,11 +102,14 @@ def tile_moe_s_glu_sigmoid_kernel(tc, x_words, x_scales, w, w3, offs, out):
             )
             return slot_words, slot_scales
 
-        def round_columns(copy, step, cols):
+        def round_into(copy, step, cols, source):
             copy(
                 out=grouped_ring[step % GROUPED_RING][:, cols, :].rearrange("p (c i) j -> p c j i", i=RUN),
-                in_=raw_pass(step)[:, :, cols].rearrange("p j (c i) -> p c j i", i=RUN),
+                in_=source.rearrange("p j (c i) -> p c j i", i=RUN),
             )
+
+        def round_columns(copy, step, cols):
+            round_into(copy, step, cols, raw_pass(step)[:, :, cols])
 
         def quantize_columns(step, cols):
             nc.vector.quantize_mx(
@@ -139,7 +142,15 @@ def tile_moe_s_glu_sigmoid_kernel(tc, x_words, x_scales, w, w3, offs, out):
         def gate_step(e):
             return step_of[(e, 0, PASSES - 1)] + 1
 
+        tail_cols = [slice(first * TAIL_COLS, last * TAIL_COLS) for first, last in TAIL_LOADS]
+        tail_raw = [
+            keep.tile([P, PACK, cols.stop - cols.start], F32, name=f"tail_raw{i}", align_bytes=256)
+            for i, cols in enumerate(tail_cols)
+        ]
+
         def gate_tile(e):
+            if e == E - 1:
+                return tail_raw[1][:].rearrange("p j n -> p (j n)")
             return raw_pass(gate_step(e))[:, 0, :]
 
         def make_gate(e):
@@ -152,9 +163,7 @@ def tile_moe_s_glu_sigmoid_kernel(tc, x_words, x_scales, w, w3, offs, out):
                 out=results[:, e, cols], in0=sums[:], in1=gate_tile(e)[:, cols], op=mybir.AluOpType.mult
             )
 
-        starts = {step_of[(first, which, 0)]: (first, last, which) for first, last in GROUPS for which in range(2)}
-        load_group(*starts[0])
-        slots = [gather_slots(part) for part in range(SLOTS // GATHER)]
+        slots = []
 
         def finish_matrix(step):
             e, which, s = work[step]
@@ -164,6 +173,8 @@ def tile_moe_s_glu_sigmoid_kernel(tc, x_words, x_scales, w, w3, offs, out):
                 apply_gate(e, sum_ring[step // PASSES % SUM_RING], slice(0, N))
 
         for step in range(STEPS - PASSES):
+            if step % (2 * PASSES * EXPERTS_PER_GATHER) == 0:
+                slots.append(gather_slots(len(slots)))
             if step > 0 and step in starts:
                 load_group(*starts[step])
             quantize_pass(step)
@@ -172,17 +183,28 @@ def tile_moe_s_glu_sigmoid_kernel(tc, x_words, x_scales, w, w3, offs, out):
                 finish_matrix(step - 1)
 
         load_group(*starts[STEPS - PASSES])
+        last_rows = w3[E - 1, K - K_PASS :, :].rearrange("(p j) n -> p j n", j=PACK)
+        for piece, cols in zip(tail_raw, tail_cols):
+            nc.sync.dma_start(out=piece[:], in_=last_rows[:, :, cols])
         nc.sync.dma_start(out=out_rows[:, : E - 1, :], in_=results[:, : E - 1, :])
         parts = [slice(g * TAIL_COLS, (g + 1) * TAIL_COLS) for g in range(TAIL_PARTS)]
-        quantize_pass(STEPS - 2)
+        last = STEPS - 1
+        round_columns(nc.vector.tensor_copy, last - 1, slice(0, VECTOR_COLS))
+        round_columns(nc.scalar.copy, last - 1, slice(VECTOR_COLS, N))
+        round_into(nc.vector.tensor_copy, last, parts[0], tail_raw[0][:, :, parts[0]])
+        round_into(nc.scalar.copy, last, parts[1], tail_raw[0][:, :, parts[1]])
+        quantize_columns(last - 1, slice(0, N))
         for g, cols in enumerate(parts):
-            multiply(tail_sums[g], slots, STEPS - 2, cols)
+            multiply(tail_sums[g], slots, last - 1, cols)
+        round_into(nc.scalar.copy, last, parts[2], tail_raw[1][:])
+        quantize_columns(last, tail_cols[0])
+        for g in (0, 1):
+            multiply(tail_sums[g], slots, last, parts[g])
         make_gate(E - 1)
-        for g, cols in enumerate(parts):
-            round_columns(nc.vector.tensor_copy if g < TAIL_VECTOR_PARTS else nc.scalar.copy, STEPS - 1, cols)
-        for g in (0, 2, 1, 3):
-            quantize_columns(STEPS - 1, parts[g])
-            multiply(tail_sums[g], slots, STEPS - 1, parts[g])
-        for g in (0, 2, 1, 3):
+        round_into(nc.vector.tensor_copy, last, parts[3], tail_raw[2][:])
+        for g in (2, 3):
+            quantize_columns(last, parts[g])
+            multiply(tail_sums[g], slots, last, parts[g])
+        for g in range(TAIL_PARTS):
             apply_gate(E - 1, tail_sums[g], parts[g])
         nc.sync.dma_start(out=out_rows[:, E - 1, :], in_=results[:, E - 1, :])

@@ -207,4 +207,5 @@ def tile_moe_s_glu_sigmoid_kernel(tc, x_words, x_scales, w, w3, offs, out):
             multiply(tail_sums[g], slots, last, parts[g])
         for g in range(TAIL_PARTS):
             apply_gate(E - 1, tail_sums[g], parts[g])
-        nc.sync.dma_start(out=out_rows[:, E - 1, :], in_=results[:, E - 1, :])
+        for cols in (slice(0, N - TAIL_COLS), parts[-1]):
+            nc.sync.dma_start(out=out_rows[:, E - 1, cols], in_=results[:, E - 1, cols])

@@ -31,6 +31,7 @@ GROUPS = tuple((e, e + 1) for e in range(E))
 GROUPED_RING = 6
 CODE_RING = 6
 SUM_RING = 4
+LONG_RUN_EXPERTS = 5
 STEPS = E * 2 * PASSES
 
 
@@ -66,8 +67,12 @@ def tile_moe_s_glu_sigmoid_kernel(tc, x_words, x_scales, w, w3, offs, out):
         def load_group(first, last, which):
             rows = (w, w3)[which][first:last].rearrange("e (s p j) n -> p (e s) j n", s=PASSES, j=PACK)
             slot = step_of[(first, which, 0)] % RAW_SLOTS
-            if last < E:
-                nc.sync.dma_start(out=raw[:, slot : slot + PASSES * (last - first)], in_=rows)
+            if LONG_RUN_EXPERTS < last < E:
+                nc.sync.dma_start(out=raw[:, slot : slot + PASSES], in_=rows)
+            elif last < E:
+                for s in range(PASSES):
+                    runs = (w, w3)[which][first, s * K_PASS : (s + 1) * K_PASS, :].rearrange("(g r) n -> g (r n)", g=32)
+                    nc.sync.dma_start(out=raw[:, slot + s].rearrange("p j n -> p (j n)"), in_=runs)
             else:
                 for s in range(PASSES - which):
                     nc.sync.dma_start(out=raw[:, slot + s], in_=rows[:, s])

@@ -18,21 +18,22 @@ P = 128
 PACK = 4
 K_PASS = P * PACK
 PASSES = K // K_PASS
-SLOTS = E * C
+MATRICES = 2 * E
+STEPS = MATRICES * PASSES
 GATHER = 512
 EXPERTS_PER_GATHER = GATHER // C
 VECTOR_COLS = 256
+RUN = 4
+RAW_RING = 8
+GROUPED_RING = 2
+CODE_RING = 6
+SUM_RING = 4
+PAIRED = range(RAW_RING // PASSES, MATRICES - 2)
+BY_PASS = (0, MATRICES - 2)
+AHEAD = RAW_RING // PASSES
 TAIL_COLS = 128
 TAIL_PARTS = N // TAIL_COLS
 TAIL_LOADS = ((0, 2), (2, 3), (3, 4))
-RUN = 4
-RAW_SLOTS = 18
-GROUPS = tuple((e, e + 1) for e in range(E))
-GROUPED_RING = 6
-CODE_RING = 6
-SUM_RING = 4
-LONG_RUN_EXPERTS = 5
-STEPS = E * 2 * PASSES
 
 
 def tile_moe_s_glu_sigmoid_kernel(tc, x_words, x_scales, w, w3, offs, out):
@@ -41,48 +42,39 @@ def tile_moe_s_glu_sigmoid_kernel(tc, x_words, x_scales, w, w3, offs, out):
         keep = ctx.enter_context(tc.tile_pool(name="keep", bufs=1))
         psum = ctx.enter_context(tc.psum_pool(name="psum", bufs=1))
 
-        offsets = keep.tile([P, SLOTS // 16], U16, name="offsets")
-
+        offsets = keep.tile([P, E * C // 16], U16, name="offsets")
         results = keep.tile([P, E, N], F32, name="results", align_bytes=256)
-        raw = keep.tile([P, RAW_SLOTS, PACK, N], F32, name="raw", align_bytes=256)
+        raw = keep.tile([P, RAW_RING, PACK * N], F32, name="raw", align_bytes=256)
         grouped_ring = [keep.tile([P, N, PACK], BF16, name=f"grouped{i}", align_bytes=64) for i in range(GROUPED_RING)]
         code_ring = [keep.tile([P, N], U32, name=f"codes{i}", align_bytes=64) for i in range(CODE_RING)]
         scale_ring = [keep.tile([P, N], U8, name=f"scales{i}", align_bytes=64) for i in range(CODE_RING)]
         sum_ring = [psum.tile([C, N], F32, name=f"sums{i}") for i in range(SUM_RING)]
-
         tail_sums = [psum.tile([C, TAIL_COLS], F32, name=f"tail_sums{g}") for g in range(TAIL_PARTS)]
 
-        work = [
-            (e, which, s)
-            for first, last in GROUPS
-            for which in range(2)
-            for e in range(first, last)
-            for s in range(PASSES)
-        ]
-        step_of = {item: step for step, item in enumerate(work)}
-
         def raw_pass(step):
-            return raw[:, step % RAW_SLOTS]
+            return raw[:, step % RAW_RING].rearrange("p (j n) -> p j n", j=PACK)
 
-        def load_group(first, last, which):
-            rows = (w, w3)[which][first:last].rearrange("e (s p j) n -> p (e s) j n", s=PASSES, j=PACK)
-            slot = step_of[(first, which, 0)] % RAW_SLOTS
-            if LONG_RUN_EXPERTS < last < E:
-                nc.sync.dma_start(out=raw[:, slot : slot + PASSES], in_=rows)
-            elif last < E:
+        def load_matrix(m):
+            rows = (w, w3)[m % 2][m // 2].rearrange("(s p j) n -> p s (j n)", s=PASSES, j=PACK)
+            slot = m * PASSES % RAW_RING
+            if m in PAIRED:
+                nc.sync.dma_start(out=raw[:, slot], in_=rows[:, 0])
+                nc.scalar.dma_start(out=raw[:, slot + 1], in_=rows[:, 1])
+            elif m in BY_PASS:
                 for s in range(PASSES):
-                    runs = (w, w3)[which][first, s * K_PASS : (s + 1) * K_PASS, :].rearrange("(g r) n -> g (r n)", g=32)
-                    nc.sync.dma_start(out=raw[:, slot + s].rearrange("p j n -> p (j n)"), in_=runs)
-            else:
-                for s in range(PASSES - which):
                     nc.sync.dma_start(out=raw[:, slot + s], in_=rows[:, s])
+            elif m < MATRICES - 1:
+                nc.sync.dma_start(out=raw[:, slot : slot + PASSES], in_=rows)
+            else:
+                nc.sync.dma_start(out=raw[:, slot], in_=rows[:, 0])
+                last_rows = rows[:, 1].rearrange("p (j n) -> p j n", j=PACK)
+                for piece, cols in zip(tail_raw, tail_cols):
+                    nc.sync.dma_start(out=piece, in_=last_rows[:, :, cols])
 
         token_words = keep.tile([P, T], I32, name="token_words", align_bytes=256)
         nc.sync.dma_start(out=token_words[:], in_=x_words[0].rearrange("p t d -> p (t d)").bitcast(I32))
         nc.sync.dma_start(offsets[:], offs)
-
-        starts = {step_of[(first, which, 0)]: (first, last, which) for first, last in GROUPS for which in range(2)}
-        load_group(*starts[0])
+        load_matrix(0)
 
         token_scales = keep.tile([P, PASSES * T], U8, name="token_scales", align_bytes=256)
         nc.vector.memset(token_scales[:].bitcast(I32), 0)
@@ -92,6 +84,9 @@ def tile_moe_s_glu_sigmoid_kernel(tc, x_words, x_scales, w, w3, offs, out):
                 out=scale_rows[32 * quadrant : 32 * quadrant + 4],
                 in_=x_scales[:, 4 * quadrant : 4 * quadrant + 4, :].bitcast(I32).rearrange("s b t -> b s t"),
             )
+
+        for m in range(1, AHEAD):
+            load_matrix(m)
 
         def gather_slots(part):
             picked = offsets[:, part * GATHER // 16 : (part + 1) * GATHER // 16]
@@ -113,8 +108,9 @@ def tile_moe_s_glu_sigmoid_kernel(tc, x_words, x_scales, w, w3, offs, out):
                 in_=source.rearrange("p j (c i) -> p c j i", i=RUN),
             )
 
-        def round_columns(copy, step, cols):
-            round_into(copy, step, cols, raw_pass(step)[:, :, cols])
+        def round_pass(step):
+            for copy, cols in ((nc.vector.tensor_copy, slice(0, VECTOR_COLS)), (nc.scalar.copy, slice(VECTOR_COLS, N))):
+                round_into(copy, step, cols, raw_pass(step)[:, :, cols])
 
         def quantize_columns(step, cols):
             nc.vector.quantize_mx(
@@ -123,13 +119,10 @@ def tile_moe_s_glu_sigmoid_kernel(tc, x_words, x_scales, w, w3, offs, out):
                 in_=grouped_ring[step % GROUPED_RING][:, cols, :].rearrange("p n j -> p (n j)"),
             )
 
-        def quantize_pass(step):
-            round_columns(nc.vector.tensor_copy, step, slice(0, VECTOR_COLS))
-            round_columns(nc.scalar.copy, step, slice(VECTOR_COLS, N))
-            quantize_columns(step, slice(0, N))
+        slots = []
 
-        def multiply(sums, slots, step, cols):
-            e, which, s = work[step]
+        def multiply(sums, step, cols):
+            e, s = step // (2 * PASSES), step % PASSES
             slot_words, slot_scales = slots[e // EXPERTS_PER_GATHER]
             first = (e % EXPERTS_PER_GATHER) * C
             nc.tensor.matmul_mx(
@@ -142,25 +135,22 @@ def tile_moe_s_glu_sigmoid_kernel(tc, x_words, x_scales, w, w3, offs, out):
                 stop=(s == PASSES - 1),
             )
 
-        out_rows = out.rearrange("(e u) n -> u e n", u=C)
-
-        def gate_step(e):
-            return step_of[(e, 0, PASSES - 1)] + 1
-
-        tail_cols = [slice(first * TAIL_COLS, last * TAIL_COLS) for first, last in TAIL_LOADS]
+        last = STEPS - 1
+        parts = [slice(g * TAIL_COLS, (g + 1) * TAIL_COLS) for g in range(TAIL_PARTS)]
+        tail_cols = [slice(first * TAIL_COLS, end * TAIL_COLS) for first, end in TAIL_LOADS]
         tail_raw = [
-            keep.tile([P, PACK, cols.stop - cols.start], F32, name=f"tail_raw{i}", align_bytes=256)
-            for i, cols in enumerate(tail_cols)
+            raw[:, last % RAW_RING, PACK * cols.start : PACK * cols.stop].rearrange("p (j n) -> p j n", j=PACK)
+            for cols in tail_cols
         ]
 
         def gate_tile(e):
             if e == E - 1:
-                return tail_raw[1][:].rearrange("p j n -> p (j n)")
-            return raw_pass(gate_step(e))[:, 0, :]
+                return tail_raw[1].rearrange("p j n -> p (j n)")
+            return results[:, e, :]
 
         def make_gate(e):
             nc.scalar.activation(
-                out=gate_tile(e), in_=sum_ring[step_of[(e, 0, 0)] // PASSES % SUM_RING][:], func=mybir.ActivationFunctionType.Sigmoid
+                out=gate_tile(e), in_=sum_ring[2 * e % SUM_RING][:], func=mybir.ActivationFunctionType.Sigmoid
             )
 
         def apply_gate(e, sums, cols):
@@ -168,48 +158,38 @@ def tile_moe_s_glu_sigmoid_kernel(tc, x_words, x_scales, w, w3, offs, out):
                 out=results[:, e, cols], in0=sums[:], in1=gate_tile(e)[:, cols], op=mybir.AluOpType.mult
             )
 
-        slots = []
-
-        def finish_matrix(step):
-            e, which, s = work[step]
-            if which == 0:
-                make_gate(e)
-            else:
-                apply_gate(e, sum_ring[step // PASSES % SUM_RING], slice(0, N))
-
         for step in range(STEPS - PASSES):
+            m = step // PASSES
             if step % (2 * PASSES * EXPERTS_PER_GATHER) == 0:
                 slots.append(gather_slots(len(slots)))
-            if step > 0 and step in starts:
-                load_group(*starts[step])
-            quantize_pass(step)
-            multiply(sum_ring[step // PASSES % SUM_RING], slots, step, slice(0, N))
+            round_pass(step)
+            if step % PASSES == PASSES - 1 and m + AHEAD < MATRICES:
+                load_matrix(m + AHEAD)
+            quantize_columns(step, slice(0, N))
+            multiply(sum_ring[m % SUM_RING], step, slice(0, N))
             if step > 0 and step % PASSES == 0:
-                finish_matrix(step - 1)
+                if m % 2 == 1:
+                    make_gate(m // 2)
+                else:
+                    apply_gate(m // 2 - 1, sum_ring[(m - 1) % SUM_RING], slice(0, N))
 
-        load_group(*starts[STEPS - PASSES])
-        last_rows = w3[E - 1, K - K_PASS :, :].rearrange("(p j) n -> p j n", j=PACK)
-        for piece, cols in zip(tail_raw, tail_cols):
-            nc.sync.dma_start(out=piece[:], in_=last_rows[:, :, cols])
+        out_rows = out.rearrange("(e u) n -> u e n", u=C)
         nc.sync.dma_start(out=out_rows[:, : E - 1, :], in_=results[:, : E - 1, :])
-        parts = [slice(g * TAIL_COLS, (g + 1) * TAIL_COLS) for g in range(TAIL_PARTS)]
-        last = STEPS - 1
-        round_columns(nc.vector.tensor_copy, last - 1, slice(0, VECTOR_COLS))
-        round_columns(nc.scalar.copy, last - 1, slice(VECTOR_COLS, N))
+        round_pass(last - 1)
         round_into(nc.vector.tensor_copy, last, parts[0], tail_raw[0][:, :, parts[0]])
         round_into(nc.scalar.copy, last, parts[1], tail_raw[0][:, :, parts[1]])
         quantize_columns(last - 1, slice(0, N))
         for g, cols in enumerate(parts):
-            multiply(tail_sums[g], slots, last - 1, cols)
-        round_into(nc.scalar.copy, last, parts[2], tail_raw[1][:])
+            multiply(tail_sums[g], last - 1, cols)
+        round_into(nc.scalar.copy, last, parts[2], tail_raw[1])
         quantize_columns(last, tail_cols[0])
         for g in (0, 1):
-            multiply(tail_sums[g], slots, last, parts[g])
+            multiply(tail_sums[g], last, parts[g])
         make_gate(E - 1)
-        round_into(nc.vector.tensor_copy, last, parts[3], tail_raw[2][:])
+        round_into(nc.vector.tensor_copy, last, parts[3], tail_raw[2])
         for g in (2, 3):
             quantize_columns(last, parts[g])
-            multiply(tail_sums[g], slots, last, parts[g])
+            multiply(tail_sums[g], last, parts[g])
         for g in range(TAIL_PARTS):
             apply_gate(E - 1, tail_sums[g], parts[g])
         for cols in (slice(0, N - TAIL_COLS), parts[-1]):

@@ -16,24 +16,20 @@ FP4X4 = mybir.dt.float4_e2m1fn_x4
 
 P = 128
 PACK = 4
-K_PASS = P * PACK
-PASSES = K // K_PASS
+PASSES = K // (P * PACK)
 MATRICES = 2 * E
-STEPS = MATRICES * PASSES
 GATHER = 512
 EXPERTS_PER_GATHER = GATHER // C
-VECTOR_COLS = 256
 RUN = 4
 RAW_RING = 8
-GROUPED_RING = 2
-CODE_RING = 6
+CODE_RING = 4
 SUM_RING = 4
-PAIRED = range(RAW_RING // PASSES, MATRICES - 2)
-BY_PASS = (0, MATRICES - 2)
-AHEAD = RAW_RING // PASSES
-TAIL_COLS = 128
-TAIL_PARTS = N // TAIL_COLS
-TAIL_LOADS = ((0, 2), (2, 3), (3, 4))
+SHARED_FROM = MATRICES - 3
+WHOLE = (1, 2, 3, 4)
+VECTOR_COLS = 256
+SCALAR_COLS = N - VECTOR_COLS
+PART = 128
+PIECES = ((0, 2), (2, 3), (3, 4))
 
 
 def tile_moe_s_glu_sigmoid_kernel(tc, x_words, x_scales, w, w3, offs, out):
@@ -44,31 +40,35 @@ def tile_moe_s_glu_sigmoid_kernel(tc, x_words, x_scales, w, w3, offs, out):
 
         offsets = keep.tile([P, E * C // 16], U16, name="offsets")
         results = keep.tile([P, E, N], F32, name="results", align_bytes=256)
-        raw = keep.tile([P, RAW_RING, PACK * N], F32, name="raw", align_bytes=256)
-        grouped_ring = [keep.tile([P, N, PACK], BF16, name=f"grouped{i}", align_bytes=64) for i in range(GROUPED_RING)]
-        code_ring = [keep.tile([P, N], U32, name=f"codes{i}", align_bytes=64) for i in range(CODE_RING)]
-        scale_ring = [keep.tile([P, N], U8, name=f"scales{i}", align_bytes=64) for i in range(CODE_RING)]
+        raw = keep.tile([P, RAW_RING, PASSES, PACK * N], F32, name="raw", align_bytes=256)
+        staging = keep.tile([P, 3 * N, PACK], BF16, name="staging", align_bytes=64)
+        code_ring = [keep.tile([P, PASSES * N], U32, name=f"codes{i}", align_bytes=64) for i in range(CODE_RING)]
+        scale_ring = [keep.tile([P, PASSES * N], U8, name=f"scales{i}", align_bytes=64) for i in range(CODE_RING)]
         sum_ring = [psum.tile([C, N], F32, name=f"sums{i}") for i in range(SUM_RING)]
-        tail_sums = [psum.tile([C, TAIL_COLS], F32, name=f"tail_sums{g}") for g in range(TAIL_PARTS)]
 
-        def raw_pass(step):
-            return raw[:, step % RAW_RING].rearrange("p (j n) -> p j n", j=PACK)
+        last = MATRICES - 1
+        piece_cols = [slice(first * PART, end * PART) for first, end in PIECES]
+        piece_raw = [
+            raw[:, last % RAW_RING, 1, PACK * cols.start : PACK * cols.stop].rearrange("p (j n) -> p j n", j=PACK)
+            for cols in piece_cols
+        ]
+
+        piece_sums = [
+            psum.tile([C, cols.stop - cols.start], F32, name=f"piece_sums{g}") for g, cols in enumerate(piece_cols)
+        ]
 
         def load_matrix(m):
             rows = (w, w3)[m % 2][m // 2].rearrange("(s p j) n -> p s (j n)", s=PASSES, j=PACK)
-            slot = m * PASSES % RAW_RING
-            if m in PAIRED:
-                nc.sync.dma_start(out=raw[:, slot], in_=rows[:, 0])
-                nc.scalar.dma_start(out=raw[:, slot + 1], in_=rows[:, 1])
-            elif m in BY_PASS:
+            slot = raw[:, m % RAW_RING]
+            if m in WHOLE:
+                nc.sync.dma_start(out=slot, in_=rows)
+            elif m < last:
                 for s in range(PASSES):
-                    nc.sync.dma_start(out=raw[:, slot + s], in_=rows[:, s])
-            elif m < MATRICES - 1:
-                nc.sync.dma_start(out=raw[:, slot : slot + PASSES], in_=rows)
+                    nc.sync.dma_start(out=slot[:, s], in_=rows[:, s])
             else:
-                nc.sync.dma_start(out=raw[:, slot], in_=rows[:, 0])
+                nc.sync.dma_start(out=slot[:, 0], in_=rows[:, 0])
                 last_rows = rows[:, 1].rearrange("p (j n) -> p j n", j=PACK)
-                for piece, cols in zip(tail_raw, tail_cols):
+                for piece, cols in zip(piece_raw, piece_cols):
                     nc.sync.dma_start(out=piece, in_=last_rows[:, :, cols])
 
         token_words = keep.tile([P, T], I32, name="token_words", align_bytes=256)
@@ -84,8 +84,7 @@ def tile_moe_s_glu_sigmoid_kernel(tc, x_words, x_scales, w, w3, offs, out):
                 out=scale_rows[32 * quadrant : 32 * quadrant + 4],
                 in_=x_scales[:, 4 * quadrant : 4 * quadrant + 4, :].bitcast(I32).rearrange("s b t -> b s t"),
             )
-
-        for m in range(1, AHEAD):
+        for m in range(1, RAW_RING):
             load_matrix(m)
 
         def gather_slots(part):
@@ -102,51 +101,58 @@ def tile_moe_s_glu_sigmoid_kernel(tc, x_words, x_scales, w, w3, offs, out):
             )
             return slot_words, slot_scales
 
-        def round_into(copy, step, cols, source):
+        def round_into(copy, at, source):
+            width = source.shape[2]
             copy(
-                out=grouped_ring[step % GROUPED_RING][:, cols, :].rearrange("p (c i) j -> p c j i", i=RUN),
+                out=staging[:, at : at + width, :].rearrange("p (c i) j -> p c j i", i=RUN),
                 in_=source.rearrange("p j (c i) -> p c j i", i=RUN),
             )
 
-        def round_pass(step):
-            for copy, cols in ((nc.vector.tensor_copy, slice(0, VECTOR_COLS)), (nc.scalar.copy, slice(VECTOR_COLS, N))):
-                round_into(copy, step, cols, raw_pass(step)[:, :, cols])
+        def raw_pass(m, s):
+            return raw[:, m % RAW_RING, s].rearrange("p (j n) -> p j n", j=PACK)
 
-        def quantize_columns(step, cols):
+        def code_cols(m, s, cols):
+            first = N * ((s + m) % PASSES if m < SHARED_FROM else s)
+            return slice(first + cols.start, first + cols.stop)
+
+        def quantize(m, at, cols):
             nc.vector.quantize_mx(
-                out=code_ring[step % CODE_RING][:, cols].bitcast(FP8X4),
-                scales=scale_ring[step % CODE_RING][:, cols],
-                in_=grouped_ring[step % GROUPED_RING][:, cols, :].rearrange("p n j -> p (n j)"),
+                out=code_ring[m % CODE_RING][:, cols].bitcast(FP8X4),
+                scales=scale_ring[m % CODE_RING][:, cols],
+                in_=staging[:, at : at + cols.stop - cols.start, :].rearrange("p n j -> p (n j)"),
             )
+
+        def round_shared(m, s):
+            source = raw_pass(m, s)
+            if s == 0:
+                round_into(nc.vector.tensor_copy, N, source[:, :, SCALAR_COLS:])
+                round_into(nc.scalar.copy, N - SCALAR_COLS, source[:, :, :SCALAR_COLS])
+                return N - SCALAR_COLS
+            round_into(nc.vector.tensor_copy, N, source[:, :, :VECTOR_COLS])
+            round_into(nc.scalar.copy, N + VECTOR_COLS, source[:, :, VECTOR_COLS:])
+            return N
 
         slots = []
 
-        def multiply(sums, step, cols):
-            e, s = step // (2 * PASSES), step % PASSES
+        def multiply(sums, m, s, cols):
+            e = m // 2
             slot_words, slot_scales = slots[e // EXPERTS_PER_GATHER]
             first = (e % EXPERTS_PER_GATHER) * C
             nc.tensor.matmul_mx(
                 out=sums[:],
                 lhsT=slot_words[:, s, 2 * first : 2 * (first + C)].bitcast(FP4X4),
                 lhsT_scale=slot_scales[:, s, first : first + C],
-                rhs=code_ring[step % CODE_RING][:, cols].bitcast(FP8X4),
-                rhs_scale=scale_ring[step % CODE_RING][:, cols],
+                rhs=code_ring[m % CODE_RING][:, code_cols(m, s, cols)].bitcast(FP8X4),
+                rhs_scale=scale_ring[m % CODE_RING][:, code_cols(m, s, cols)],
                 start=(s == 0),
                 stop=(s == PASSES - 1),
             )
 
-        last = STEPS - 1
-        parts = [slice(g * TAIL_COLS, (g + 1) * TAIL_COLS) for g in range(TAIL_PARTS)]
-        tail_cols = [slice(first * TAIL_COLS, end * TAIL_COLS) for first, end in TAIL_LOADS]
-        tail_raw = [
-            raw[:, last % RAW_RING, PACK * cols.start : PACK * cols.stop].rearrange("p (j n) -> p j n", j=PACK)
-            for cols in tail_cols
-        ]
-
         def gate_tile(e):
             if e == E - 1:
-                return tail_raw[1].rearrange("p j n -> p (j n)")
-            return results[:, e, :]
+                return piece_raw[1].rearrange("p j n -> p (j n)")
+            after = 2 * e + 2
+            return raw[:, after % RAW_RING, 1 if after < SHARED_FROM else 0, PACK * N - N :]
 
         def make_gate(e):
             nc.scalar.activation(
@@ -158,39 +164,54 @@ def tile_moe_s_glu_sigmoid_kernel(tc, x_words, x_scales, w, w3, offs, out):
                 out=results[:, e, cols], in0=sums[:], in1=gate_tile(e)[:, cols], op=mybir.AluOpType.mult
             )
 
-        for step in range(STEPS - PASSES):
-            m = step // PASSES
-            if step % (2 * PASSES * EXPERTS_PER_GATHER) == 0:
+        def finish_expert(e):
+            make_gate(e)
+            apply_gate(e, sum_ring[(2 * e + 1) % SUM_RING], slice(0, N))
+
+        whole = slice(0, N)
+        for m in range(last):
+            if m % (2 * EXPERTS_PER_GATHER) == 0:
                 slots.append(gather_slots(len(slots)))
-            round_pass(step)
-            if step % PASSES == PASSES - 1 and m + AHEAD < MATRICES:
-                load_matrix(m + AHEAD)
-            quantize_columns(step, slice(0, N))
-            multiply(sum_ring[m % SUM_RING], step, slice(0, N))
-            if step > 0 and step % PASSES == 0:
-                if m % 2 == 1:
-                    make_gate(m // 2)
-                else:
-                    apply_gate(m // 2 - 1, sum_ring[(m - 1) % SUM_RING], slice(0, N))
+            if m < SHARED_FROM:
+                round_into(nc.scalar.copy, 2 * N * (m % 2), raw_pass(m, 0))
+                round_into(nc.vector.tensor_copy, N, raw_pass(m, 1))
+                quantize(m, N * (m % 2), slice(0, PASSES * N))
+                if m > 0 and m % 2 == 0:
+                    finish_expert(m // 2 - 1)
+                if m + RAW_RING < MATRICES:
+                    load_matrix(m + RAW_RING)
+                for s in range(PASSES):
+                    multiply(sum_ring[m % SUM_RING], m, s, whole)
+            else:
+                for s in range(PASSES):
+                    at = round_shared(m, s)
+                    quantize(m, at, code_cols(m, s, whole))
+                    if s == 0 and m % 2 == 0:
+                        finish_expert(m // 2 - 1)
+                    multiply(sum_ring[m % SUM_RING], m, s, whole)
 
         out_rows = out.rearrange("(e u) n -> u e n", u=C)
         nc.sync.dma_start(out=out_rows[:, : E - 1, :], in_=results[:, : E - 1, :])
-        round_pass(last - 1)
-        round_into(nc.vector.tensor_copy, last, parts[0], tail_raw[0][:, :, parts[0]])
-        round_into(nc.scalar.copy, last, parts[1], tail_raw[0][:, :, parts[1]])
-        quantize_columns(last - 1, slice(0, N))
-        for g, cols in enumerate(parts):
-            multiply(tail_sums[g], last - 1, cols)
-        round_into(nc.scalar.copy, last, parts[2], tail_raw[1])
-        quantize_columns(last, tail_cols[0])
-        for g in (0, 1):
-            multiply(tail_sums[g], last, parts[g])
+        at = round_shared(last, 0)
+        halves = (slice(0, N // 2), slice(N // 2, N))
+        for half in reversed(halves):
+            quantize(last, at + half.start, half)
+        for g in (1, 2, 0):
+            multiply(piece_sums[g], last, 0, piece_cols[g])
+        piece_at = (at + N - PART, 2 * N, at)
+
+        def quantize_piece(g):
+            quantize(last, piece_at[g], code_cols(last, 1, piece_cols[g]))
+            multiply(piece_sums[g], last, 1, piece_cols[g])
+
+        round_into(nc.vector.tensor_copy, piece_at[0], piece_raw[0][:, :, :PART])
+        round_into(nc.scalar.copy, piece_at[0] + PART, piece_raw[0][:, :, PART:])
+        round_into(nc.scalar.copy, piece_at[1], piece_raw[1])
+        quantize_piece(0)
         make_gate(E - 1)
-        round_into(nc.vector.tensor_copy, last, parts[3], tail_raw[2])
-        for g in (2, 3):
-            quantize_columns(last, parts[g])
-            multiply(tail_sums[g], last, parts[g])
-        for g in range(TAIL_PARTS):
-            apply_gate(E - 1, tail_sums[g], parts[g])
-        for cols in (slice(0, N - TAIL_COLS), parts[-1]):
+        round_into(nc.vector.tensor_copy, piece_at[2], piece_raw[2])
+        quantize_piece(1)
+        quantize_piece(2)
+        for sums, cols in zip(piece_sums, piece_cols):
+            apply_gate(E - 1, sums, cols)
             nc.sync.dma_start(out=out_rows[:, E - 1, cols], in_=results[:, E - 1, cols])

@@ -24,7 +24,7 @@ RUN = 4
 RAW_RING = 8
 CODE_RING = 4
 SUM_RING = 4
-SHARED_FROM = MATRICES - 3
+SHARED_FROM = MATRICES - 5
 WHOLE = (1, 2, 3, 4)
 VECTOR_COLS = 256
 SCALAR_COLS = N - VECTOR_COLS
@@ -214,4 +214,5 @@ def tile_moe_s_glu_sigmoid_kernel(tc, x_words, x_scales, w, w3, offs, out):
         quantize_piece(2)
         for sums, cols in zip(piece_sums, piece_cols):
             apply_gate(E - 1, sums, cols)
+        for cols in (slice(0, N - PART), piece_cols[-1]):
             nc.sync.dma_start(out=out_rows[:, E - 1, cols], in_=results[:, E - 1, cols])

@@ -29,6 +29,7 @@ WHOLE = (1, 2, 3, 4)
 VECTOR_COLS = 256
 SCALAR_COLS = N - VECTOR_COLS
 PART = 128
+FIRST_VECTOR_COLS = 160
 PIECES = ((0, 2), (2, 3), (3, 4))
 
 
@@ -36,26 +37,26 @@ def tile_moe_s_glu_sigmoid_kernel(tc, x_words, x_scales, w, w3, offs, out):
     nc = tc.nc
     with ExitStack() as ctx:
         keep = ctx.enter_context(tc.tile_pool(name="keep", bufs=1))
+        shared = ctx.enter_context(tc.tile_pool(name="shared", bufs=1))
         psum = ctx.enter_context(tc.psum_pool(name="psum", bufs=1))
 
         offsets = keep.tile([P, E * C // 16], U16, name="offsets")
-        results = keep.tile([P, E, N], F32, name="results", align_bytes=256)
+        results = keep.tile([P, E - 1, N], F32, name="results", align_bytes=256)
         raw = keep.tile([P, RAW_RING, PASSES, PACK * N], F32, name="raw", align_bytes=256)
-        staging = keep.tile([P, 3 * N, PACK], BF16, name="staging", align_bytes=64)
+        staging = shared.tile([P, 3 * N, PACK], BF16, name="staging", align_bytes=256, offset=0)
+        last_results = shared.tile([P, N], F32, name="last_results", align_bytes=256, offset=0)
         code_ring = [keep.tile([P, PASSES * N], U32, name=f"codes{i}", align_bytes=64) for i in range(CODE_RING)]
         scale_ring = [keep.tile([P, PASSES * N], U8, name=f"scales{i}", align_bytes=64) for i in range(CODE_RING)]
         sum_ring = [psum.tile([C, N], F32, name=f"sums{i}") for i in range(SUM_RING)]
 
         last = MATRICES - 1
         piece_cols = [slice(first * PART, end * PART) for first, end in PIECES]
-        piece_raw = [
-            raw[:, last % RAW_RING, 1, PACK * cols.start : PACK * cols.stop].rearrange("p (j n) -> p j n", j=PACK)
-            for cols in piece_cols
-        ]
-
         piece_sums = [
             psum.tile([C, cols.stop - cols.start], F32, name=f"piece_sums{g}") for g, cols in enumerate(piece_cols)
         ]
+
+        def raw_pass(m, s):
+            return raw[:, m % RAW_RING, s].rearrange("p (j n) -> p j n", j=PACK)
 
         def load_matrix(m):
             rows = (w, w3)[m % 2][m // 2].rearrange("(s p j) n -> p s (j n)", s=PASSES, j=PACK)
@@ -67,9 +68,12 @@ def tile_moe_s_glu_sigmoid_kernel(tc, x_words, x_scales, w, w3, offs, out):
                     nc.sync.dma_start(out=slot[:, s], in_=rows[:, s])
             else:
                 nc.sync.dma_start(out=slot[:, 0], in_=rows[:, 0])
+                half = piece_cols[0].stop
+                for run in (slice(0, 2 * N + half), slice(3 * N, 3 * N + half)):
+                    nc.sync.dma_start(out=slot[:, 1, run], in_=rows[:, 1, run])
                 last_rows = rows[:, 1].rearrange("p (j n) -> p j n", j=PACK)
-                for piece, cols in zip(piece_raw, piece_cols):
-                    nc.sync.dma_start(out=piece, in_=last_rows[:, :, cols])
+                for cols in piece_cols[1:]:
+                    nc.sync.dma_start(out=raw_pass(m, 1)[:, 2:, cols], in_=last_rows[:, 2:, cols])
 
         token_words = keep.tile([P, T], I32, name="token_words", align_bytes=256)
         nc.sync.dma_start(out=token_words[:], in_=x_words[0].rearrange("p t d -> p (t d)").bitcast(I32))
@@ -107,9 +111,6 @@ def tile_moe_s_glu_sigmoid_kernel(tc, x_words, x_scales, w, w3, offs, out):
                 out=staging[:, at : at + width, :].rearrange("p (c i) j -> p c j i", i=RUN),
                 in_=source.rearrange("p j (c i) -> p c j i", i=RUN),
             )
-
-        def raw_pass(m, s):
-            return raw[:, m % RAW_RING, s].rearrange("p (j n) -> p j n", j=PACK)
 
         def code_cols(m, s, cols):
             first = N * ((s + m) % PASSES if m < SHARED_FROM else s)
@@ -149,8 +150,6 @@ def tile_moe_s_glu_sigmoid_kernel(tc, x_words, x_scales, w, w3, offs, out):
             )
 
         def gate_tile(e):
-            if e == E - 1:
-                return piece_raw[1].rearrange("p j n -> p (j n)")
             after = 2 * e + 2
             return raw[:, after % RAW_RING, 1 if after < SHARED_FROM else 0, PACK * N - N :]
 
@@ -191,28 +190,40 @@ def tile_moe_s_glu_sigmoid_kernel(tc, x_words, x_scales, w, w3, offs, out):
                     multiply(sum_ring[m % SUM_RING], m, s, whole)
 
         out_rows = out.rearrange("(e u) n -> u e n", u=C)
-        nc.sync.dma_start(out=out_rows[:, : E - 1, :], in_=results[:, : E - 1, :])
+        nc.sync.dma_start(out=out_rows[:, : E - 1, :], in_=results[:])
         at = round_shared(last, 0)
         halves = (slice(0, N // 2), slice(N // 2, N))
         for half in reversed(halves):
             quantize(last, at + half.start, half)
         for g in (1, 2, 0):
             multiply(piece_sums[g], last, 0, piece_cols[g])
-        piece_at = (at + N - PART, 2 * N, at)
-
-        def quantize_piece(g):
-            quantize(last, piece_at[g], code_cols(last, 1, piece_cols[g]))
+        source = raw_pass(last, 1)
+        first_at, second_at = at + N - PART, at + N + PART
+        first_gate = raw_pass(last, 0)[:, 0, : N // 2]
+        second_gate = source[:, :2, piece_cols[2]]
+        gate_sums = sum_ring[(last - 1) % SUM_RING]
+        sigmoid = mybir.ActivationFunctionType.Sigmoid
+        nc.scalar.activation(out=first_gate, in_=gate_sums[:, halves[0]], func=sigmoid)
+        round_into(nc.vector.tensor_copy, first_at, source[:, :, :FIRST_VECTOR_COLS])
+        round_into(nc.scalar.copy, first_at + FIRST_VECTOR_COLS, source[:, :, FIRST_VECTOR_COLS : 2 * PART])
+        round_into(nc.vector.tensor_copy, second_at, source[:, :, piece_cols[1]])
+        round_into(nc.scalar.copy, second_at + PART, source[:, :, piece_cols[2]])
+        nc.scalar.activation(
+            out=second_gate, in_=gate_sums[:, halves[1]].rearrange("p (g c) -> p g c", g=2), func=sigmoid
+        )
+        for cols in piece_cols:
+            quantize(last, first_at + cols.start, code_cols(last, 1, cols))
+        for g in range(len(PIECES)):
             multiply(piece_sums[g], last, 1, piece_cols[g])
-
-        round_into(nc.vector.tensor_copy, piece_at[0], piece_raw[0][:, :, :PART])
-        round_into(nc.scalar.copy, piece_at[0] + PART, piece_raw[0][:, :, PART:])
-        round_into(nc.scalar.copy, piece_at[1], piece_raw[1])
-        quantize_piece(0)
-        make_gate(E - 1)
-        round_into(nc.vector.tensor_copy, piece_at[2], piece_raw[2])
-        quantize_piece(1)
-        quantize_piece(2)
-        for sums, cols in zip(piece_sums, piece_cols):
-            apply_gate(E - 1, sums, cols)
+        nc.vector.tensor_tensor(
+            out=last_results[:, halves[0]], in0=piece_sums[0][:], in1=first_gate, op=mybir.AluOpType.mult
+        )
+        for g in (1, 2):
+            nc.vector.tensor_tensor(
+                out=last_results[:, piece_cols[g]],
+                in0=piece_sums[g][:],
+                in1=second_gate[:, g - 1],
+                op=mybir.AluOpType.mult,
+            )
         for cols in (slice(0, N - PART), piece_cols[-1]):
-            nc.sync.dma_start(out=out_rows[:, E - 1, cols], in_=results[:, E - 1, cols])
+            nc.sync.dma_start(out=out_rows[:, E - 1, cols], in_=last_results[:, cols])

@@ -68,12 +68,9 @@ def tile_moe_s_glu_sigmoid_kernel(tc, x_words, x_scales, w, w3, offs, out):
                     nc.sync.dma_start(out=slot[:, s], in_=rows[:, s])
             else:
                 nc.sync.dma_start(out=slot[:, 0], in_=rows[:, 0])
-                half = piece_cols[0].stop
-                for run in (slice(0, 2 * N + half), slice(3 * N, 3 * N + half)):
-                    nc.sync.dma_start(out=slot[:, 1, run], in_=rows[:, 1, run])
-                last_rows = rows[:, 1].rearrange("p (j n) -> p j n", j=PACK)
-                for cols in piece_cols[1:]:
-                    nc.sync.dma_start(out=raw_pass(m, 1)[:, 2:, cols], in_=last_rows[:, 2:, cols])
+                pairs = [ap[:, 1].rearrange("p (i f) -> p i f", i=2) for ap in (slot, rows)]
+                for first, end in ((0, N + piece_cols[0].stop),) + tuple((N + c.start, N + c.stop) for c in piece_cols[1:]):
+                    nc.sync.dma_start(out=pairs[0][:, :, first:end], in_=pairs[1][:, :, first:end])
 
         token_words = keep.tile([P, T], I32, name="token_words", align_bytes=256)
         nc.sync.dma_start(out=token_words[:], in_=x_words[0].rearrange("p t d -> p (t d)").bitcast(I32))
@@ -225,5 +222,5 @@ def tile_moe_s_glu_sigmoid_kernel(tc, x_words, x_scales, w, w3, offs, out):
                 in1=second_gate[:, g - 1],
                 op=mybir.AluOpType.mult,
             )
-        for cols in (slice(0, N - PART), piece_cols[-1]):
+        for cols in piece_cols:
             nc.sync.dma_start(out=out_rows[:, E - 1, cols], in_=last_results[:, cols])

from contextlib import ExitStack

import concourse.mybir as mybir

K, T, E, C, N = 1024, 1024, 8, 128, 512
FLOPS = 2 * 2 * E * C * K * N

F32 = mybir.dt.float32
BF16 = mybir.dt.bfloat16
I32 = mybir.dt.int32
U32 = mybir.dt.uint32
U16 = mybir.dt.uint16
U8 = mybir.dt.uint8
FP8X4 = mybir.dt.float8_e4m3fn_x4
FP4X4 = mybir.dt.float4_e2m1fn_x4

P = 128
PACK = 4
PASSES = K // (P * PACK)
MATRICES = 2 * E
GATHER = 512
EXPERTS_PER_GATHER = GATHER // C
RUN = 4
RAW_RING = 8
CODE_RING = 4
SUM_RING = 4
SHARED_FROM = MATRICES - 5
WHOLE = (1, 2, 3, 4)
VECTOR_COLS = 256
SCALAR_COLS = N - VECTOR_COLS
PART = 128
FIRST_VECTOR_COLS = 160
PIECES = ((0, 2), (2, 3), (3, 4))


def tile_moe_s_glu_sigmoid_kernel(tc, x_words, x_scales, w, w3, offs, out):
    nc = tc.nc
    with ExitStack() as ctx:
        keep = ctx.enter_context(tc.tile_pool(name="keep", bufs=1))
        shared = ctx.enter_context(tc.tile_pool(name="shared", bufs=1))
        psum = ctx.enter_context(tc.psum_pool(name="psum", bufs=1))

        offsets = keep.tile([P, E * C // 16], U16, name="offsets")
        results = keep.tile([P, E - 1, N], F32, name="results", align_bytes=256)
        raw = keep.tile([P, RAW_RING, PASSES, PACK * N], F32, name="raw", align_bytes=256)
        staging = shared.tile([P, 3 * N, PACK], BF16, name="staging", align_bytes=256, offset=0)
        last_results = shared.tile([P, N], F32, name="last_results", align_bytes=256, offset=0)
        code_ring = [keep.tile([P, PASSES * N], U32, name=f"codes{i}", align_bytes=64) for i in range(CODE_RING)]
        scale_ring = [keep.tile([P, PASSES * N], U8, name=f"scales{i}", align_bytes=64) for i in range(CODE_RING)]
        sum_ring = [psum.tile([C, N], F32, name=f"sums{i}") for i in range(SUM_RING)]

        last = MATRICES - 1
        piece_cols = [slice(first * PART, end * PART) for first, end in PIECES]
        piece_sums = [
            psum.tile([C, cols.stop - cols.start], F32, name=f"piece_sums{g}") for g, cols in enumerate(piece_cols)
        ]

        def raw_pass(m, s):
            return raw[:, m % RAW_RING, s].rearrange("p (j n) -> p j n", j=PACK)

        def load_matrix(m):
            rows = (w, w3)[m % 2][m // 2].rearrange("(s p j) n -> p s (j n)", s=PASSES, j=PACK)
            slot = raw[:, m % RAW_RING]
            if m in WHOLE:
                nc.sync.dma_start(out=slot, in_=rows)
            elif m < last:
                for s in range(PASSES):
                    nc.sync.dma_start(out=slot[:, s], in_=rows[:, s])
            else:
                nc.sync.dma_start(out=slot[:, 0], in_=rows[:, 0])
                pairs = [ap[:, 1].rearrange("p (i f) -> p i f", i=2) for ap in (slot, rows)]
                for first, end in ((0, N + piece_cols[0].stop),) + tuple((N + c.start, N + c.stop) for c in piece_cols[1:]):
                    nc.sync.dma_start(out=pairs[0][:, :, first:end], in_=pairs[1][:, :, first:end])

        token_words = keep.tile([P, T], I32, name="token_words", align_bytes=256)
        nc.sync.dma_start(out=token_words[:], in_=x_words[0].rearrange("p t d -> p (t d)").bitcast(I32))
        nc.sync.dma_start(offsets[:], offs)
        load_matrix(0)

        token_scales = keep.tile([P, PASSES * T], U8, name="token_scales", align_bytes=256)
        nc.vector.memset(token_scales[:].bitcast(I32), 0)
        scale_rows = token_scales[:].bitcast(I32).rearrange("p (s t) -> p s t", s=PASSES)
        for quadrant in range(4):
            nc.sync.dma_start(
                out=scale_rows[32 * quadrant : 32 * quadrant + 4],
                in_=x_scales[:, 4 * quadrant : 4 * quadrant + 4, :].bitcast(I32).rearrange("s b t -> b s t"),
            )
        for m in range(1, RAW_RING):
            load_matrix(m)

        def gather_slots(part):
            picked = offsets[:, part * GATHER // 16 : (part + 1) * GATHER // 16]
            pair_words = keep.tile([P, GATHER], U32, name=f"pair_words{part}")
            nc.vector.tensor_copy(pair_words[:], token_words[:].bitcast(U32).indirect(picked))
            slot_scales = keep.tile([P, PASSES, GATHER], U8, name=f"slot_scales{part}", align_bytes=64)
            for s in range(PASSES):
                nc.vector.tensor_copy(slot_scales[:, s, :], token_scales[:, s * T : (s + 1) * T].indirect(picked))
            slot_words = keep.tile([P, PASSES, 2 * GATHER], U8, name=f"slot_words{part}", align_bytes=64)
            nc.vector.tensor_copy(
                slot_words[:].bitcast(U16),
                pair_words[:].bitcast(U16).rearrange("p (j s) -> p s j", s=PASSES),
            )
            return slot_words, slot_scales

        def round_into(copy, at, source):
            width = source.shape[2]
            copy(
                out=staging[:, at : at + width, :].rearrange("p (c i) j -> p c j i", i=RUN),
                in_=source.rearrange("p j (c i) -> p c j i", i=RUN),
            )

        def code_cols(m, s, cols):
            first = N * ((s + m) % PASSES if m < SHARED_FROM else s)
            return slice(first + cols.start, first + cols.stop)

        def quantize(m, at, cols):
            nc.vector.quantize_mx(
                out=code_ring[m % CODE_RING][:, cols].bitcast(FP8X4),
                scales=scale_ring[m % CODE_RING][:, cols],
                in_=staging[:, at : at + cols.stop - cols.start, :].rearrange("p n j -> p (n j)"),
            )

        def round_shared(m, s):
            source = raw_pass(m, s)
            if s == 0:
                round_into(nc.vector.tensor_copy, N, source[:, :, SCALAR_COLS:])
                round_into(nc.scalar.copy, N - SCALAR_COLS, source[:, :, :SCALAR_COLS])
                return N - SCALAR_COLS
            round_into(nc.vector.tensor_copy, N, source[:, :, :VECTOR_COLS])
            round_into(nc.scalar.copy, N + VECTOR_COLS, source[:, :, VECTOR_COLS:])
            return N

        slots = []

        def multiply(sums, m, s, cols):
            e = m // 2
            slot_words, slot_scales = slots[e // EXPERTS_PER_GATHER]
            first = (e % EXPERTS_PER_GATHER) * C
            nc.tensor.matmul_mx(
                out=sums[:],
                lhsT=slot_words[:, s, 2 * first : 2 * (first + C)].bitcast(FP4X4),
                lhsT_scale=slot_scales[:, s, first : first + C],
                rhs=code_ring[m % CODE_RING][:, code_cols(m, s, cols)].bitcast(FP8X4),
                rhs_scale=scale_ring[m % CODE_RING][:, code_cols(m, s, cols)],
                start=(s == 0),
                stop=(s == PASSES - 1),
            )

        def gate_tile(e):
            after = 2 * e + 2
            return raw[:, after % RAW_RING, 1 if after < SHARED_FROM else 0, PACK * N - N :]

        def make_gate(e):
            nc.scalar.activation(
                out=gate_tile(e), in_=sum_ring[2 * e % SUM_RING][:], func=mybir.ActivationFunctionType.Sigmoid
            )

        def apply_gate(e, sums, cols):
            nc.vector.tensor_tensor(
                out=results[:, e, cols], in0=sums[:], in1=gate_tile(e)[:, cols], op=mybir.AluOpType.mult
            )

        def finish_expert(e):
            make_gate(e)
            apply_gate(e, sum_ring[(2 * e + 1) % SUM_RING], slice(0, N))

        whole = slice(0, N)
        for m in range(last):
            if m % (2 * EXPERTS_PER_GATHER) == 0:
                slots.append(gather_slots(len(slots)))
            if m < SHARED_FROM:
                round_into(nc.scalar.copy, 2 * N * (m % 2), raw_pass(m, 0))
                round_into(nc.vector.tensor_copy, N, raw_pass(m, 1))
                quantize(m, N * (m % 2), slice(0, PASSES * N))
                if m > 0 and m % 2 == 0:
                    finish_expert(m // 2 - 1)
                if m + RAW_RING < MATRICES:
                    load_matrix(m + RAW_RING)
                for s in range(PASSES):
                    multiply(sum_ring[m % SUM_RING], m, s, whole)
            else:
                for s in range(PASSES):
                    at = round_shared(m, s)
                    quantize(m, at, code_cols(m, s, whole))
                    if s == 0 and m % 2 == 0:
                        finish_expert(m // 2 - 1)
                    multiply(sum_ring[m % SUM_RING], m, s, whole)

        out_rows = out.rearrange("(e u) n -> u e n", u=C)
        nc.sync.dma_start(out=out_rows[:, : E - 1, :], in_=results[:])
        at = round_shared(last, 0)
        halves = (slice(0, N // 2), slice(N // 2, N))
        for half in reversed(halves):
            quantize(last, at + half.start, half)
        for g in (1, 2, 0):
            multiply(piece_sums[g], last, 0, piece_cols[g])
        source = raw_pass(last, 1)
        first_at, second_at = at + N - PART, at + N + PART
        first_gate = raw_pass(last, 0)[:, 0, : N // 2]
        second_gate = source[:, :2, piece_cols[2]]
        gate_sums = sum_ring[(last - 1) % SUM_RING]
        sigmoid = mybir.ActivationFunctionType.Sigmoid
        nc.scalar.activation(out=first_gate, in_=gate_sums[:, halves[0]], func=sigmoid)
        round_into(nc.vector.tensor_copy, first_at, source[:, :, :FIRST_VECTOR_COLS])
        round_into(nc.scalar.copy, first_at + FIRST_VECTOR_COLS, source[:, :, FIRST_VECTOR_COLS : 2 * PART])
        round_into(nc.vector.tensor_copy, second_at, source[:, :, piece_cols[1]])
        round_into(nc.scalar.copy, second_at + PART, source[:, :, piece_cols[2]])
        nc.scalar.activation(
            out=second_gate, in_=gate_sums[:, halves[1]].rearrange("p (g c) -> p g c", g=2), func=sigmoid
        )
        for cols in piece_cols:
            quantize(last, first_at + cols.start, code_cols(last, 1, cols))
        for g in range(len(PIECES)):
            multiply(piece_sums[g], last, 1, piece_cols[g])
        nc.vector.tensor_tensor(
            out=last_results[:, halves[0]], in0=piece_sums[0][:], in1=first_gate, op=mybir.AluOpType.mult
        )
        for g in (1, 2):
            nc.vector.tensor_tensor(
                out=last_results[:, piece_cols[g]],
                in0=piece_sums[g][:],
                in1=second_gate[:, g - 1],
                op=mybir.AluOpType.mult,
            )
        for cols in piece_cols:
            nc.sync.dma_start(out=out_rows[:, E - 1, cols], in_=last_results[:, cols])
